import numpy as np
import ml_dtypes


def mxq(x, axis, fmt="e4m3"):
    dtype, down = {"e4m3": (ml_dtypes.float8_e4m3fn, 7), "e5m2": (ml_dtypes.float8_e5m2, 14)}[fmt]
    v = np.moveaxis(np.asarray(x, np.float32).astype(ml_dtypes.bfloat16).astype(np.float64), axis, -1)
    blocks = v.reshape(v.shape[:-1] + (-1, 32))
    amax = np.abs(blocks).max(-1, keepdims=True)
    byte = np.maximum(np.where(amax > 0, np.frexp(amax)[1] - 1 + 127, 0) - down, 1)
    scale = np.exp2(byte - 127.0)
    codes = (blocks / scale).astype(np.float32).astype(dtype).astype(np.float64)
    return np.moveaxis((codes * scale).reshape(v.shape), -1, axis)


WIDE = False


def mx_kscale(k):
    if not WIDE:
        return np.ones(k)
    levels = np.array([10, -10, 5, -5, 0])
    if k % 512:
        return np.exp2(np.random.permutation(np.resize(levels, k // 32))).repeat(32)
    a = np.empty((k // 512, 16))
    for p in range(k // 512):
        a[p, :8] = np.random.permutation(np.resize(levels, 8))
        for g in range(8):
            far = levels[np.abs(levels - a[p, g]) >= 10]
            a[p, g + 8] = far[np.random.randint(len(far))]
    return np.exp2(a.ravel()).repeat(32)


BF16 = ml_dtypes.bfloat16


def bf(x):
    return np.asarray(x, np.float32).astype(BF16)


def f64(x):
    return np.asarray(x).astype(np.float64)


B, D, T, P, Q = 32, 512, 512, 128, 128


def scaled_softmax(e):
    p = np.exp(e - e.max(axis=-1, keepdims=True))
    return e.shape[-1] * (p / p.sum(axis=-1, keepdims=True))


def draw0():
    s, t = mx_kscale(D), mx_kscale(T)
    return {
        "x": bf(np.random.standard_normal((B, D, T)) * s[None, :, None]),
        "w1": bf(np.random.standard_normal((P, D)) / np.sqrt(D) / s[None, :]),
        "g": bf((1.0 + 0.1 * np.random.standard_normal(T)) * t),
        "w": bf(np.random.standard_normal((T, Q)) / np.sqrt(T) / t[:, None]),
        "w2": bf(np.random.standard_normal((T, Q)) / np.sqrt(T) / t[:, None]),
        "lam": bf(np.random.uniform(0.3, 0.7, P)),
        "bias": bf(0.4 * np.random.standard_normal((P, Q))),
    }


def core(x, w1, g, w, w2, lam, bias):
    h0 = mxq(f64(w1), 1, "e4m3") @ mxq(f64(x), 1, "e4m3")
    h = h0 * f64(g)[None, None, :]
    hq = mxq(h, 2, "e4m3")
    u = hq @ mxq(f64(w2), 0, "e4m3")
    e = hq @ mxq(f64(w), 0, "e4m3")
    a = scaled_softmax(e)
    mix = f64(lam)[None, :, None]
    z = mix * u * a + (1.0 - mix) * u + f64(bias)[None, :, :]
    return np.tanh(z)


def e4m3fn_bytes(y):
    return np.clip(np.asarray(y, np.float64), -448.0, 448.0).astype(np.float32).astype(ml_dtypes.float8_e4m3fn).view(np.uint8)


def e4m3fn_values(b):
    return np.asarray(b, np.uint8).view(ml_dtypes.float8_e4m3fn).astype(np.float64)


def setup_inputs():
    d = draw0()
    x0 = np.asarray(d['x']).astype(np.float64)
    s = (np.max(np.abs(x0), axis=(0, 2), keepdims=True) / 448.0).astype(np.float32)
    out = {}
    for k, v in d.items():
        if k == 'x':
            out['x_bytes'] = e4m3fn_bytes(x0 / s.astype(np.float64))
            out['x_scale'] = s
        else:
            out[k] = v
    return out


def reference(x_bytes, x_scale, w1, g, w, w2, lam, bias):
    return core(e4m3fn_values(x_bytes) * x_scale.astype(np.float64), w1, g, w, w2, lam, bias)

@@ -1,0 +1,319 @@
+from contextlib import ExitStack
+
+import concourse.mybir as mybir
+from concourse.masks import make_identity
+
+B, D, T, PF, Q = 32, 512, 512, 128, 128
+FLOPS = 2 * B * PF * D * T + 2 * 2 * B * PF * T * Q
+
+F32 = mybir.dt.float32
+BF16 = mybir.dt.bfloat16
+U32 = mybir.dt.uint32
+U8 = mybir.dt.uint8
+FP8 = mybir.dt.float8_e4m3fn
+FP8X4 = mybir.dt.float8_e4m3fn_x4
+ALU = mybir.AluOpType
+ACT = mybir.ActivationFunctionType
+AX = mybir.AxisListType
+
+P = 128
+AHEAD = 3
+LOAD_AHEAD = 10
+GROUPS = [4] * 7 + [2, 2]
+
+
+def m_vector(n):
+    if n < 2:
+        return 128
+    if n >= 30:
+        return 72
+    return 104
+
+
+def tile_temporalaugmentedbilinear_t_kernel(tc, x_bytes, x_scale, w1, g, w, w2, lam, bias, out):
+    nc = tc.nc
+    with ExitStack() as ctx:
+        keep = ctx.enter_context(tc.tile_pool(name="keep", bufs=1))
+        raws = ctx.enter_context(tc.tile_pool(name="raws", bufs=6))
+        pln = ctx.enter_context(tc.tile_pool(name="pln", bufs=3))
+        grp = ctx.enter_context(tc.tile_pool(name="grp", bufs=3))
+        cod = ctx.enter_context(tc.tile_pool(name="cod", bufs=3))
+        hp = ctx.enter_context(tc.tile_pool(name="hp", bufs=2))
+        ep = ctx.enter_context(tc.tile_pool(name="ep", bufs=2))
+        ps_h = ctx.enter_context(tc.psum_pool(name="ps_h", bufs=3))
+        ps_u = ctx.enter_context(tc.psum_pool(name="ps_u", bufs=2))
+        ps_e = ctx.enter_context(tc.psum_pool(name="ps_e", bufs=2))
+        ctx.enter_context(tc.manual_schedule())
+
+        raw = {}
+
+        def load(b):
+            if b >= B:
+                return
+            q = b // 2
+            if b % 2 == 0:
+                raw[q] = raws.tile([P, 4, 2, T], U8, name="raw", align_bytes=64)
+            nc.sync.dma_start(out=raw[q][:, :, b % 2, :], in_=x_bytes[b].rearrange("(p i) t -> p i t", i=4))
+
+        xs = keep.tile([P, 4], F32, name="xs")
+        nc.sync.dma_start(out=xs[:], in_=x_scale.rearrange("o (p i) z -> p (o i z)", i=4))
+        load(0)
+        load(1)
+
+        w1_sb = keep.tile([P, D], BF16, name="w1_sb", align_bytes=64)
+        w_sb = keep.tile([P, 2, 4, Q], BF16, name="w_sb", align_bytes=64)
+        g_sb = keep.tile([P, 4], BF16, name="g_sb")
+        lam_sb = keep.tile([P, 1], BF16, name="lam_sb")
+        bias_sb = keep.tile([P, Q], BF16, name="bias_sb")
+        nc.scalar.dma_start(out=w1_sb[:], in_=w1)
+        nc.scalar.dma_start(out=w_sb[:, 0], in_=w2.rearrange("(p j) q -> p j q", j=4))
+        nc.scalar.dma_start(out=w_sb[:, 1], in_=w.rearrange("(p j) q -> p j q", j=4))
+        nc.scalar.dma_start(out=g_sb[:], in_=g.rearrange("(p j) -> p j", j=4))
+        nc.scalar.dma_start(out=lam_sb[:], in_=lam.rearrange("(p o) -> p o", o=1))
+        nc.scalar.dma_start(out=bias_sb[:], in_=bias)
+        for b in range(2, LOAD_AHEAD):
+            load(b)
+
+        warm = keep.tile([P, 1], F32, name="warm")
+        nc.gpsimd.memset(warm[:], 0.0)
+        nc.scalar.activation(out=warm[:], in_=warm[:], func=ACT.Exp)
+
+        ident = keep.tile([P, P], F32, name="ident")
+        make_identity(nc, ident[:])
+
+        planes = {}
+
+        def new_planes(q):
+            planes[q] = pln.tile([P, 4, 2, T], BF16, name="planes", align_bytes=64)
+
+        def widen_half(h):
+            if h >= B:
+                return
+            q = h // 2
+            if h % 2 == 0:
+                new_planes(q)
+            for i in (2 * (h % 2), 2 * (h % 2) + 1):
+                nc.scalar.activation(
+                    out=planes[q][:, i].rearrange("p b t -> p (b t)"),
+                    in_=raw[q][:, i].rearrange("p b t -> p (b t)").bitcast(FP8),
+                    func=ACT.Copy,
+                    scale=xs[:, i : i + 1],
+                )
+
+        new_planes(0)
+        for i in range(4):
+            nc.vector.tensor_scalar(
+                out=planes[0][:, i, 0, :], in0=raw[0][:, i, 0, :].bitcast(FP8),
+                scalar1=xs[:, i : i + 1], scalar2=None, op0=ALU.mult,
+            )
+        for i in range(4):
+            nc.scalar.activation(
+                out=planes[0][:, i, 1, :], in_=raw[0][:, i, 1, :].bitcast(FP8),
+                func=ACT.Copy, scale=xs[:, i : i + 1],
+            )
+        widen_half(2)
+
+        w1_words = w1_sb[:].bitcast(F32)
+        w1_t = ps_h.tile([P, 512], F32, name="h_ps")
+        for u in (0, 1):
+            nc.tensor.transpose(w1_t[:, 128 * u : 128 * (u + 1)], w1_words[:, u : 256 : 2], ident[:])
+        w1_g = keep.tile([P, 512], BF16, name="w1_g", align_bytes=64)
+        w1_c = keep.tile([P, 128], U32, name="w1_c", align_bytes=64)
+        w1_s = keep.tile([P, 128], U8, name="w1_s", align_bytes=64)
+        w_g = keep.tile([P, 2, Q, 4], BF16, name="w_g", align_bytes=64)
+        w_c = keep.tile([P, 256], U32, name="w_c", align_bytes=64)
+        w_s = keep.tile([P, 256], U8, name="w_s", align_bytes=64)
+
+        def prep_w1_copy():
+            nc.vector.tensor_copy(
+                out=w1_g[:].bitcast(F32).rearrange("p (r u) -> p r u", u=2),
+                in_=w1_t[:, 0:256].rearrange("p (u r) -> p r u", u=2),
+            )
+
+        def prep_w1_quant():
+            nc.vector.quantize_mx(out=w1_c[:].bitcast(FP8X4), scales=w1_s[:], in_=w1_g[:])
+
+        def prep_w_copy():
+            nc.vector.tensor_copy(out=w_g[:, 0], in_=w_sb[:, 0].rearrange("p j q -> p q j"))
+            nc.vector.tensor_scalar(
+                out=w_g[:, 1], in0=w_sb[:, 1].rearrange("p j q -> p q j"),
+                scalar1=-1.0, scalar2=None, op0=ALU.mult,
+            )
+
+        def prep_w_quant():
+            nc.vector.quantize_mx(
+                out=w_c[:].bitcast(FP8X4), scales=w_s[:], in_=w_g[:].rearrange("p a q j -> p (a q j)")
+            )
+
+        lam_lo = keep.tile([P, 1], F32, name="lam_lo")
+        lam_hi = keep.tile([P, 1], F32, name="lam_hi")
+        c128 = keep.tile([P, 1], F32, name="c128")
+        oml = keep.tile([P, 1], F32, name="oml")
+        rc = keep.tile([P, 1], F32, name="rc")
+        kk = keep.tile([P, 1], F32, name="kk")
+        TINY = 1e-20
+
+        def prep_lam():
+            nc.gpsimd.tensor_scalar(out=lam_lo[:], in0=lam_sb[:], scalar1=TINY, scalar2=TINY, op0=ALU.is_lt, op1=ALU.mult)
+            nc.gpsimd.tensor_scalar(out=lam_hi[:], in0=lam_sb[:], scalar1=-TINY, scalar2=None, op0=ALU.is_gt)
+            nc.gpsimd.tensor_tensor(out=lam_lo[:], in0=lam_lo[:], in1=lam_hi[:], op=ALU.mult)
+            nc.gpsimd.tensor_tensor(out=c128[:], in0=lam_lo[:], in1=lam_sb[:], op=ALU.add)
+            nc.gpsimd.tensor_scalar(out=c128[:], in0=c128[:], scalar1=128.0, scalar2=None, op0=ALU.mult)
+            nc.gpsimd.tensor_scalar(out=oml[:], in0=lam_sb[:], scalar1=-1.0, scalar2=1.0, op0=ALU.mult, op1=ALU.add)
+            nc.vector.reciprocal(rc[:], c128[:])
+            nc.gpsimd.tensor_tensor(out=kk[:], in0=oml[:], in1=rc[:], op=ALU.mult)
+
+        grouped, xc, xsc = {}, {}, {}
+
+        def interleave(n):
+            grouped[n] = grp.tile([P, 4, 128, 4], BF16, name="grouped", align_bytes=64)
+            src = planes[n // 2][:, :, n % 2, :].rearrange("p i (m j) -> p m i j", j=4)
+            dst = grouped[n][:].rearrange("p j m i -> p m i j")
+            mv = m_vector(n)
+            nc.vector.tensor_copy(out=dst[:, 0:mv], in_=src[:, 0:mv])
+            if mv < 128:
+                nc.scalar.copy(out=dst[:, mv:128], in_=src[:, mv:128])
+
+        def quant(n):
+            xc[n] = cod.tile([P, 512], U32, name="xc", align_bytes=64)
+            xsc[n] = cod.tile([P, 512], U8, name="xsc", align_bytes=64)
+            nc.vector.quantize_mx(
+                out=xc[n][:].bitcast(FP8X4), scales=xsc[n][:],
+                in_=grouped[n][:].rearrange("p j m i -> p (j m i)"),
+            )
+
+        h_ps = {}
+
+        def mm1(n):
+            h_ps[n] = ps_h.tile([P, 512], F32, name="h_ps")
+            for j in range(4):
+                cols = slice(128 * j, 128 * (j + 1))
+                nc.tensor.matmul_mx(
+                    out=h_ps[n][:, cols],
+                    lhsT=xc[n][:, cols].bitcast(FP8X4), lhsT_scale=xsc[n][:, cols],
+                    rhs=w1_c[:].bitcast(FP8X4), rhs_scale=w1_s[:],
+                    start=True, stop=True,
+                )
+
+        hg, hc, hs = {}, {}, {}
+
+        def gain(n):
+            q = n // 2
+            if n % 2 == 0:
+                hg[q] = hp.tile([P, 2, PF, 4], BF16, name="hg", align_bytes=64)
+            nc.vector.tensor_tensor(
+                out=hg[q][:, n % 2],
+                in0=h_ps[n][:].rearrange("p (j f) -> p f j", j=4),
+                in1=g_sb[:].unsqueeze(1).to_broadcast([P, PF, 4]),
+                op=ALU.mult,
+            )
+
+        def hquant(q):
+            hc[q] = hp.tile([P, 2 * PF], U32, name="hc", align_bytes=64)
+            hs[q] = hp.tile([P, 2 * PF], U8, name="hs", align_bytes=64)
+            nc.vector.quantize_mx(
+                out=hc[q][:].bitcast(FP8X4), scales=hs[q][:], in_=hg[q][:].rearrange("p b f j -> p (b f j)")
+            )
+
+        first = [sum(GROUPS[:k]) for k in range(len(GROUPS))]
+        group_of = [k for k, size in enumerate(GROUPS) for r in range(size)]
+        u_ps, e_ps = {}, {}
+
+        def mm2(q):
+            for b in (2 * q, 2 * q + 1):
+                k = group_of[b]
+                if b == first[k]:
+                    u_ps[k] = ps_u.tile([P, 4, Q], F32, name="u_ps")
+                    e_ps[k] = ps_e.tile([P, 4, Q], F32, name="e_ps")
+                rows = slice(PF * (b % 2), PF * (b % 2 + 1))
+                for dst, cols in ((u_ps[k], slice(0, Q)), (e_ps[k], slice(Q, 2 * Q))):
+                    nc.tensor.matmul_mx(
+                        out=dst[:, b - first[k], :],
+                        lhsT=hc[q][:, rows].bitcast(FP8X4), lhsT_scale=hs[q][:, rows],
+                        rhs=w_c[:, cols].bitcast(FP8X4), rhs_scale=w_s[:, cols],
+                        start=True, stop=True,
+                    )
+
+        mn, sm, rs, cc, ks, ex = {}, {}, {}, {}, {}, {}
+
+        def row_max(k):
+            s = GROUPS[k]
+            mn[k] = ep.tile([P, 4], F32, name="mn")
+            nc.vector.tensor_reduce(out=mn[k][:, 0:s], in_=e_ps[k][:, 0:s], axis=AX.X, op=ALU.min)
+
+        def exps(k):
+            sm[k] = ep.tile([P, 4], F32, name="sm")
+            ex[k] = ep.tile([P, 4, Q], F32, name="ex")
+            for r in range(GROUPS[k]):
+                nc.scalar.activation(
+                    out=ex[k][:, r], in_=e_ps[k][:, r], func=ACT.Exp,
+                    bias=mn[k][:, r : r + 1], scale=-1.0, accum_out=sm[k][:, r : r + 1],
+                )
+
+        def factors(k):
+            s = GROUPS[k]
+            rs[k] = ep.tile([P, 4], F32, name="rs")
+            cc[k] = ep.tile([P, 4], F32, name="cc")
+            ks[k] = ep.tile([P, 4], F32, name="ks")
+            nc.gpsimd.tensor_scalar(out=ks[k][:, 0:s], in0=sm[k][:, 0:s], scalar1=kk[:, 0:1], scalar2=None, op0=ALU.mult)
+            nc.vector.reciprocal(rs[k][:, 0:s], sm[k][:, 0:s])
+            nc.gpsimd.tensor_scalar(out=cc[k][:, 0:s], in0=rs[k][:, 0:s], scalar1=c128[:, 0:1], scalar2=None, op0=ALU.mult)
+
+        def weigh(k, r):
+            nc.vector.scalar_tensor_tensor(
+                out=ex[k][:, r], in0=ex[k][:, r], scalar=ks[k][:, r : r + 1], in1=u_ps[k][:, r],
+                op0=ALU.add, op1=ALU.mult,
+            )
+
+        def mix(k, r):
+            nc.vector.scalar_tensor_tensor(
+                out=ex[k][:, r], in0=ex[k][:, r], scalar=cc[k][:, r : r + 1], in1=bias_sb[:],
+                op0=ALU.mult, op1=ALU.add,
+            )
+
+        def finish(k):
+            s, b0 = GROUPS[k], first[k]
+            o = ep.tile([P, 4, Q], F32, name="o")
+            nc.scalar.activation(out=o[:, 0:s], in_=ex[k][:, 0:s], func=ACT.Tanh)
+            nc.sync.dma_start(out=out[b0 : b0 + s].rearrange("b p q -> p b q"), in_=o[:, 0:s])
+
+        vec_a, vec_b, sca = {}, {}, {}
+        for k, s in enumerate(GROUPS):
+            n0 = first[k] + s - 1 + 3
+            vec_a.setdefault(n0 + 1, []).append((row_max, (k,)))
+            sca.setdefault(n0 + 2, []).append((exps, (k,)))
+            vec_a.setdefault(n0 + 3, []).append((factors, (k,)))
+            for r in range(s):
+                (vec_a if r % 2 == 0 else vec_b).setdefault(n0 + 4, []).append((weigh, (k, r)))
+                (vec_a if r % 2 == 0 else vec_b).setdefault(n0 + 5, []).append((mix, (k, r)))
+            sca.setdefault(n0 + 6, []).append((finish, (k,)))
+
+        def run(table, n):
+            for fn, args in table.get(n, []):
+                fn(*args)
+
+        for n in range(B + 12):
+            load(n + LOAD_AHEAD)
+            if n < B:
+                interleave(n)
+            if n + AHEAD < B:
+                widen_half(n + AHEAD)
+            if n == 0:
+                prep_w1_copy()
+            run(vec_a, n)
+            if 0 <= n - 2 < B:
+                gain(n - 2)
+            if n == 0:
+                prep_w_copy()
+                prep_w1_quant()
+                prep_lam()
+            run(vec_b, n)
+            if 0 <= n - 1 < B:
+                quant(n - 1)
+                mm1(n - 1)
+            if n == 0:
+                prep_w_quant()
+            if n - 3 >= 0 and n - 3 < B and (n - 3) % 2 == 1:
+                hquant((n - 3) // 2)
+                mm2((n - 3) // 2)
+            run(sca, n)

@@ -17,17 +17,16 @@ ACT = mybir.ActivationFunctionType
 AX = mybir.AxisListType
 
 P = 128
-AHEAD = 3
+AHEAD = 5
 LOAD_AHEAD = 10
-GROUPS = [4] * 7 + [2, 2]
 
 
-def m_vector(n):
+def shares(n):
     if n < 2:
-        return 128
-    if n >= 30:
-        return 72
-    return 104
+        return 16, 0, 0, 0
+    if n >= 28:
+        return 6, 6, 2, 2
+    return 12, 0, 2, 2
 
 
 def tile_temporalaugmentedbilinear_t_kernel(tc, x_bytes, x_scale, w1, g, w, w2, lam, bias, out):
@@ -35,14 +34,14 @@ def tile_temporalaugmentedbilinear_t_kernel(tc, x_bytes, x_scale, w1, g, w, w2, 
     with ExitStack() as ctx:
         keep = ctx.enter_context(tc.tile_pool(name="keep", bufs=1))
         raws = ctx.enter_context(tc.tile_pool(name="raws", bufs=6))
-        pln = ctx.enter_context(tc.tile_pool(name="pln", bufs=3))
+        pln = ctx.enter_context(tc.tile_pool(name="pln", bufs=4))
         grp = ctx.enter_context(tc.tile_pool(name="grp", bufs=3))
         cod = ctx.enter_context(tc.tile_pool(name="cod", bufs=3))
         hp = ctx.enter_context(tc.tile_pool(name="hp", bufs=2))
-        ep = ctx.enter_context(tc.tile_pool(name="ep", bufs=2))
+        ep = ctx.enter_context(tc.tile_pool(name="ep", bufs=4))
         ps_h = ctx.enter_context(tc.psum_pool(name="ps_h", bufs=3))
-        ps_u = ctx.enter_context(tc.psum_pool(name="ps_u", bufs=2))
-        ps_e = ctx.enter_context(tc.psum_pool(name="ps_e", bufs=2))
+        ps_ue = ctx.enter_context(tc.psum_pool(name="ps_ue", bufs=3))
+        ps_i = ctx.enter_context(tc.psum_pool(name="ps_i", bufs=2))
         ctx.enter_context(tc.manual_schedule())
 
         raw = {}
@@ -66,12 +65,20 @@ def tile_temporalaugmentedbilinear_t_kernel(tc, x_bytes, x_scale, w1, g, w, w2, 
         lam_sb = keep.tile([P, 1], BF16, name="lam_sb")
         bias_sb = keep.tile([P, Q], BF16, name="bias_sb")
         nc.scalar.dma_start(out=w1_sb[:], in_=w1)
-        nc.scalar.dma_start(out=w_sb[:, 0], in_=w2.rearrange("(p j) q -> p j q", j=4))
-        nc.scalar.dma_start(out=w_sb[:, 1], in_=w.rearrange("(p j) q -> p j q", j=4))
-        nc.scalar.dma_start(out=g_sb[:], in_=g.rearrange("(p j) -> p j", j=4))
+        g_rows = keep.tile([P, P], BF16, name="g_rows", align_bytes=64)
+        nc.gpsimd.memset(g_rows[:], 0.0)
+        nc.scalar.dma_start(
+            out=g_rows[0:4, :].rearrange("j (a r) -> j a r", r=8), in_=g.rearrange("(a j r) -> j a r", j=4, r=8)
+        )
         nc.scalar.dma_start(out=lam_sb[:], in_=lam.rearrange("(p o) -> p o", o=1))
         nc.scalar.dma_start(out=bias_sb[:], in_=bias)
-        for b in range(2, LOAD_AHEAD):
+        for b in range(2, 6):
+            load(b)
+        for k, wt in enumerate((w2, w)):
+            rows = wt.rearrange("(a j r) q -> r a j q", j=4, r=8)
+            for r in range(8):
+                nc.sync.dma_start(out=w_sb[r:P:8, k], in_=rows[r])
+        for b in range(6, LOAD_AHEAD):
             load(b)
 
         warm = keep.tile([P, 1], F32, name="warm")
@@ -80,6 +87,8 @@ def tile_temporalaugmentedbilinear_t_kernel(tc, x_bytes, x_scale, w1, g, w, w2, 
 
         ident = keep.tile([P, P], F32, name="ident")
         make_identity(nc, ident[:])
+        ident_b = keep.tile([P, P], BF16, name="ident_b", align_bytes=64)
+        nc.gpsimd.tensor_copy(out=ident_b[:], in_=ident[:])
 
         planes = {}
 
@@ -111,7 +120,8 @@ def tile_temporalaugmentedbilinear_t_kernel(tc, x_bytes, x_scale, w1, g, w, w2, 
                 out=planes[0][:, i, 1, :], in_=raw[0][:, i, 1, :].bitcast(FP8),
                 func=ACT.Copy, scale=xs[:, i : i + 1],
             )
-        widen_half(2)
+        for h in range(2, AHEAD):
+            widen_half(h)
 
         w1_words = w1_sb[:].bitcast(F32)
         w1_t = ps_h.tile([P, 512], F32, name="h_ps")
@@ -124,7 +134,11 @@ def tile_temporalaugmentedbilinear_t_kernel(tc, x_bytes, x_scale, w1, g, w, w2, 
         w_c = keep.tile([P, 256], U32, name="w_c", align_bytes=64)
         w_s = keep.tile([P, 256], U8, name="w_s", align_bytes=64)
 
+        g_t = ps_i.tile([P, P], BF16, name="id_ps")
+        nc.tensor.transpose(g_t[:], g_rows[:], ident_b[:])
+
         def prep_w1_copy():
+            nc.vector.tensor_copy(out=g_sb[:], in_=g_t[:, 0:4])
             nc.vector.tensor_copy(
                 out=w1_g[:].bitcast(F32).rearrange("p (r u) -> p r u", u=2),
                 in_=w1_t[:, 0:256].rearrange("p (u r) -> p r u", u=2),
@@ -165,21 +179,57 @@ def tile_temporalaugmentedbilinear_t_kernel(tc, x_bytes, x_scale, w1, g, w, w2, 
 
         grouped, xc, xsc = {}, {}, {}
 
-        def interleave(n):
-            grouped[n] = grp.tile([P, 4, 128, 4], BF16, name="grouped", align_bytes=64)
-            src = planes[n // 2][:, :, n % 2, :].rearrange("p i (m j) -> p m i j", j=4)
-            dst = grouped[n][:].rearrange("p j m i -> p m i j")
-            mv = m_vector(n)
-            nc.vector.tensor_copy(out=dst[:, 0:mv], in_=src[:, 0:mv])
-            if mv < 128:
-                nc.scalar.copy(out=dst[:, mv:128], in_=src[:, mv:128])
+        def lay(n, part):
+            s = shares(n)
+            a0 = sum(s[:part])
+            a1 = a0 + s[part]
+            src = planes[n // 2][:, :, n % 2, :].rearrange("p i (a j r) -> p a j r i", j=4, r=8)
+            dst = grouped[n][:].rearrange("p j a r i -> p a j r i")
+            return src[:, a0:a1], dst[:, a0:a1]
+
+        def interleave_g(n):
+            if n >= B:
+                return
+            grouped[n] = grp.tile([P, 4, 16, 8, 4], BF16, name="grouped", align_bytes=64)
+            if shares(n)[3]:
+                src, dst = lay(n, 3)
+                nc.gpsimd.tensor_scalar(out=dst, in0=src, scalar1=1.0, scalar2=0.0, op0=ALU.mult, op1=ALU.add)
+
+        def interleave_v(n):
+            src, dst = lay(n, 0)
+            nc.vector.tensor_copy(out=dst, in_=src)
+
+        id_ps = {}
+
+        def interleave_t(n):
+            if n >= B or not shares(n)[2]:
+                return
+            src, dst = lay(n, 2)
+            id_ps[n] = ps_i.tile([P, 256], BF16, name="id_ps")
+            nc.tensor.matmul(
+                id_ps[n][:].rearrange("p (t i) -> p t i", i=4), lhsT=ident_b[:],
+                rhs=src.rearrange("p a j r i -> p (a j r) i"), start=True, stop=True,
+            )
+
+        def interleave_s(n):
+            if n >= B:
+                return
+            if shares(n)[2]:
+                src, dst = lay(n, 2)
+                nc.scalar.copy(
+                    out=dst.rearrange("p a j r i -> p a j (r i)"),
+                    in_=id_ps[n][:].rearrange("p (a j c) -> p a j c", j=4, c=32),
+                )
+            if shares(n)[1]:
+                src, dst = lay(n, 1)
+                nc.scalar.copy(out=dst, in_=src)
 
         def quant(n):
             xc[n] = cod.tile([P, 512], U32, name="xc", align_bytes=64)
             xsc[n] = cod.tile([P, 512], U8, name="xsc", align_bytes=64)
             nc.vector.quantize_mx(
                 out=xc[n][:].bitcast(FP8X4), scales=xsc[n][:],
-                in_=grouped[n][:].rearrange("p j m i -> p (j m i)"),
+                in_=grouped[n][:].rearrange("p j a r i -> p (j a r i)"),
             )
 
         h_ps = {}
@@ -215,105 +265,94 @@ def tile_temporalaugmentedbilinear_t_kernel(tc, x_bytes, x_scale, w1, g, w, w2, 
                 out=hc[q][:].bitcast(FP8X4), scales=hs[q][:], in_=hg[q][:].rearrange("p b f j -> p (b f j)")
             )
 
-        first = [sum(GROUPS[:k]) for k in range(len(GROUPS))]
-        group_of = [k for k, size in enumerate(GROUPS) for r in range(size)]
-        u_ps, e_ps = {}, {}
+        ue = {}
 
         def mm2(q):
-            for b in (2 * q, 2 * q + 1):
-                k = group_of[b]
-                if b == first[k]:
-                    u_ps[k] = ps_u.tile([P, 4, Q], F32, name="u_ps")
-                    e_ps[k] = ps_e.tile([P, 4, Q], F32, name="e_ps")
-                rows = slice(PF * (b % 2), PF * (b % 2 + 1))
-                for dst, cols in ((u_ps[k], slice(0, Q)), (e_ps[k], slice(Q, 2 * Q))):
-                    nc.tensor.matmul_mx(
-                        out=dst[:, b - first[k], :],
-                        lhsT=hc[q][:, rows].bitcast(FP8X4), lhsT_scale=hs[q][:, rows],
-                        rhs=w_c[:, cols].bitcast(FP8X4), rhs_scale=w_s[:, cols],
-                        start=True, stop=True,
-                    )
+            ue[q] = ps_ue.tile([P, 2, 2, Q], F32, name="ue")
+            for r in (0, 1):
+                rows = slice(PF * r, PF * (r + 1))
+                nc.tensor.matmul_mx(
+                    out=ue[q][:, r].rearrange("p a q -> p (a q)"),
+                    lhsT=hc[q][:, rows].bitcast(FP8X4), lhsT_scale=hs[q][:, rows],
+                    rhs=w_c[:].bitcast(FP8X4), rhs_scale=w_s[:],
+                    start=True, stop=True,
+                )
 
         mn, sm, rs, cc, ks, ex = {}, {}, {}, {}, {}, {}
 
-        def row_max(k):
-            s = GROUPS[k]
-            mn[k] = ep.tile([P, 4], F32, name="mn")
-            nc.vector.tensor_reduce(out=mn[k][:, 0:s], in_=e_ps[k][:, 0:s], axis=AX.X, op=ALU.min)
+        def row_max(q):
+            mn[q] = ep.tile([P, 2], F32, name="mn")
+            nc.vector.tensor_reduce(out=mn[q][:], in_=ue[q][:, :, 1], axis=AX.X, op=ALU.min)
 
-        def exps(k):
-            sm[k] = ep.tile([P, 4], F32, name="sm")
-            ex[k] = ep.tile([P, 4, Q], F32, name="ex")
-            for r in range(GROUPS[k]):
+        def exps(q):
+            sm[q] = ep.tile([P, 2], F32, name="sm")
+            ex[q] = ep.tile([P, 2, Q], F32, name="ex")
+            for r in (0, 1):
                 nc.scalar.activation(
-                    out=ex[k][:, r], in_=e_ps[k][:, r], func=ACT.Exp,
-                    bias=mn[k][:, r : r + 1], scale=-1.0, accum_out=sm[k][:, r : r + 1],
+                    out=ex[q][:, r], in_=ue[q][:, r, 1], func=ACT.Exp,
+                    bias=mn[q][:, r : r + 1], scale=-1.0, accum_out=sm[q][:, r : r + 1],
                 )
 
-        def factors(k):
-            s = GROUPS[k]
-            rs[k] = ep.tile([P, 4], F32, name="rs")
-            cc[k] = ep.tile([P, 4], F32, name="cc")
-            ks[k] = ep.tile([P, 4], F32, name="ks")
-            nc.gpsimd.tensor_scalar(out=ks[k][:, 0:s], in0=sm[k][:, 0:s], scalar1=kk[:, 0:1], scalar2=None, op0=ALU.mult)
-            nc.vector.reciprocal(rs[k][:, 0:s], sm[k][:, 0:s])
-            nc.gpsimd.tensor_scalar(out=cc[k][:, 0:s], in0=rs[k][:, 0:s], scalar1=c128[:, 0:1], scalar2=None, op0=ALU.mult)
+        def factors(q):
+            rs[q] = ep.tile([P, 2], F32, name="rs")
+            cc[q] = ep.tile([P, 2], F32, name="cc")
+            ks[q] = ep.tile([P, 2], F32, name="ks")
+            nc.gpsimd.tensor_scalar(out=ks[q][:], in0=sm[q][:], scalar1=kk[:, 0:1], scalar2=None, op0=ALU.mult)
+            nc.vector.reciprocal(rs[q][:], sm[q][:])
+            nc.gpsimd.tensor_scalar(out=cc[q][:], in0=rs[q][:], scalar1=c128[:, 0:1], scalar2=None, op0=ALU.mult)
 
-        def weigh(k, r):
-            nc.vector.scalar_tensor_tensor(
-                out=ex[k][:, r], in0=ex[k][:, r], scalar=ks[k][:, r : r + 1], in1=u_ps[k][:, r],
-                op0=ALU.add, op1=ALU.mult,
-            )
+        def weigh(q):
+            for r in (0, 1):
+                nc.vector.scalar_tensor_tensor(
+                    out=ex[q][:, r], in0=ex[q][:, r], scalar=ks[q][:, r : r + 1], in1=ue[q][:, r, 0],
+                    op0=ALU.add, op1=ALU.mult,
+                )
 
-        def mix(k, r):
-            nc.vector.scalar_tensor_tensor(
-                out=ex[k][:, r], in0=ex[k][:, r], scalar=cc[k][:, r : r + 1], in1=bias_sb[:],
-                op0=ALU.mult, op1=ALU.add,
-            )
+        def mix(q):
+            for r in (0, 1):
+                nc.vector.scalar_tensor_tensor(
+                    out=ex[q][:, r], in0=ex[q][:, r], scalar=cc[q][:, r : r + 1], in1=bias_sb[:],
+                    op0=ALU.mult, op1=ALU.add,
+                )
 
-        def finish(k):
-            s, b0 = GROUPS[k], first[k]
-            o = ep.tile([P, 4, Q], F32, name="o")
-            nc.scalar.activation(out=o[:, 0:s], in_=ex[k][:, 0:s], func=ACT.Tanh)
-            nc.sync.dma_start(out=out[b0 : b0 + s].rearrange("b p q -> p b q"), in_=o[:, 0:s])
+        def finish(q):
+            o = ep.tile([P, 2, Q], F32, name="o")
+            nc.scalar.activation(out=o[:], in_=ex[q][:], func=ACT.Tanh)
+            nc.sync.dma_start(out=out[2 * q : 2 * q + 2].rearrange("b p q -> p b q"), in_=o[:])
 
-        vec_a, vec_b, sca = {}, {}, {}
-        for k, s in enumerate(GROUPS):
-            n0 = first[k] + s - 1 + 3
-            vec_a.setdefault(n0 + 1, []).append((row_max, (k,)))
-            sca.setdefault(n0 + 2, []).append((exps, (k,)))
-            vec_a.setdefault(n0 + 3, []).append((factors, (k,)))
-            for r in range(s):
-                (vec_a if r % 2 == 0 else vec_b).setdefault(n0 + 4, []).append((weigh, (k, r)))
-                (vec_a if r % 2 == 0 else vec_b).setdefault(n0 + 5, []).append((mix, (k, r)))
-            sca.setdefault(n0 + 6, []).append((finish, (k,)))
+        def at(stage, lag, n):
+            if 0 <= n - lag < B and (n - lag) % 2 == 0:
+                stage((n - lag) // 2)
 
-        def run(table, n):
-            for fn, args in table.get(n, []):
-                fn(*args)
-
-        for n in range(B + 12):
+        interleave_g(0)
+        interleave_g(1)
+        for n in range(B + 9):
             load(n + LOAD_AHEAD)
             if n < B:
-                interleave(n)
-            if n + AHEAD < B:
-                widen_half(n + AHEAD)
+                interleave_v(n)
             if n == 0:
                 prep_w1_copy()
-            run(vec_a, n)
-            if 0 <= n - 2 < B:
-                gain(n - 2)
-            if n == 0:
-                prep_w_copy()
                 prep_w1_quant()
                 prep_lam()
-            run(vec_b, n)
+            if n == 2:
+                prep_w_copy()
+            if n == 3:
+                prep_w_quant()
             if 0 <= n - 1 < B:
                 quant(n - 1)
                 mm1(n - 1)
-            if n == 0:
-                prep_w_quant()
-            if n - 3 >= 0 and n - 3 < B and (n - 3) % 2 == 1:
-                hquant((n - 3) // 2)
-                mm2((n - 3) // 2)
-            run(sca, n)
+            interleave_g(n + 2)
+            interleave_t(n + 2)
+            interleave_s(n + 1)
+            if n + AHEAD < B:
+                widen_half(n + AHEAD)
+            if 0 <= n - 2 < B:
+                gain(n - 2)
+            at(weigh, 8, n)
+            at(row_max, 5, n)
+            at(mix, 9, n)
+            at(factors, 7, n)
+            at(exps, 6, n)
+            at(hquant, 4, n)
+            at(mm2, 4, n)
+            at(finish, 10, n)

@@ -23,10 +23,10 @@ LOAD_AHEAD = 10
 
 def shares(n):
     if n < 2:
-        return 16, 0, 0, 0
+        return 32, 0, 0, 0
     if n >= 28:
-        return 6, 6, 2, 2
-    return 12, 0, 2, 2
+        return 2, 20, 4, 6
+    return 22, 0, 4, 6
 
 
 def tile_temporalaugmentedbilinear_t_kernel(tc, x_bytes, x_scale, w1, g, w, w2, lam, bias, out):
@@ -68,16 +68,16 @@ def tile_temporalaugmentedbilinear_t_kernel(tc, x_bytes, x_scale, w1, g, w, w2, 
         g_rows = keep.tile([P, P], BF16, name="g_rows", align_bytes=64)
         nc.gpsimd.memset(g_rows[:], 0.0)
         nc.scalar.dma_start(
-            out=g_rows[0:4, :].rearrange("j (a r) -> j a r", r=8), in_=g.rearrange("(a j r) -> j a r", j=4, r=8)
+            out=g_rows[0:4, :].rearrange("j (s r) -> j s r", r=4), in_=g.rearrange("(s j r) -> j s r", j=4, r=4)
         )
         nc.scalar.dma_start(out=lam_sb[:], in_=lam.rearrange("(p o) -> p o", o=1))
         nc.scalar.dma_start(out=bias_sb[:], in_=bias)
         for b in range(2, 6):
             load(b)
         for k, wt in enumerate((w2, w)):
-            rows = wt.rearrange("(a j r) q -> r a j q", j=4, r=8)
-            for r in range(8):
-                nc.sync.dma_start(out=w_sb[r:P:8, k], in_=rows[r])
+            rows = wt.rearrange("(s j r) q -> r s j q", j=4, r=4)
+            for r in range(4):
+                nc.sync.dma_start(out=w_sb[r:P:4, k], in_=rows[r])
         for b in range(6, LOAD_AHEAD):
             load(b)
 
@@ -102,24 +102,26 @@ def tile_temporalaugmentedbilinear_t_kernel(tc, x_bytes, x_scale, w1, g, w, w2, 
             if h % 2 == 0:
                 new_planes(q)
             for i in (2 * (h % 2), 2 * (h % 2) + 1):
-                nc.scalar.activation(
-                    out=planes[q][:, i].rearrange("p b t -> p (b t)"),
-                    in_=raw[q][:, i].rearrange("p b t -> p (b t)").bitcast(FP8),
-                    func=ACT.Copy,
-                    scale=xs[:, i : i + 1],
-                )
+                wide = planes[q][:, i].rearrange("p b t -> p (b t)")
+                codes = raw[q][:, i].rearrange("p b t -> p (b t)").bitcast(FP8)
+                if i == 3 and q % 3 == 2:
+                    nc.vector.tensor_scalar(out=wide, in0=codes, scalar1=xs[:, i : i + 1], scalar2=None, op0=ALU.mult)
+                else:
+                    nc.scalar.activation(out=wide, in_=codes, func=ACT.Copy, scale=xs[:, i : i + 1])
 
         new_planes(0)
-        for i in range(4):
-            nc.vector.tensor_scalar(
-                out=planes[0][:, i, 0, :], in0=raw[0][:, i, 0, :].bitcast(FP8),
-                scalar1=xs[:, i : i + 1], scalar2=None, op0=ALU.mult,
-            )
-        for i in range(4):
-            nc.scalar.activation(
-                out=planes[0][:, i, 1, :], in_=raw[0][:, i, 1, :].bitcast(FP8),
-                func=ACT.Copy, scale=xs[:, i : i + 1],
-            )
+        for b in (0, 1):
+            for i in range(4):
+                if i < 2:
+                    nc.vector.tensor_scalar(
+                        out=planes[0][:, i, b, :], in0=raw[0][:, i, b, :].bitcast(FP8),
+                        scalar1=xs[:, i : i + 1], scalar2=None, op0=ALU.mult,
+                    )
+                else:
+                    nc.scalar.activation(
+                        out=planes[0][:, i, b, :], in_=raw[0][:, i, b, :].bitcast(FP8),
+                        func=ACT.Copy, scale=xs[:, i : i + 1],
+                    )
         for h in range(2, AHEAD):
             widen_half(h)
 
@@ -183,20 +185,20 @@ def tile_temporalaugmentedbilinear_t_kernel(tc, x_bytes, x_scale, w1, g, w, w2, 
             s = shares(n)
             a0 = sum(s[:part])
             a1 = a0 + s[part]
-            src = planes[n // 2][:, :, n % 2, :].rearrange("p i (a j r) -> p a j r i", j=4, r=8)
-            dst = grouped[n][:].rearrange("p j a r i -> p a j r i")
+            src = planes[n // 2][:, :, n % 2, :].rearrange("p i (s j r) -> p s j r i", j=4, r=4)
+            dst = grouped[n][:].rearrange("p j s r i -> p s j r i")
             return src[:, a0:a1], dst[:, a0:a1]
 
         def interleave_g(n):
             if n >= B:
                 return
-            grouped[n] = grp.tile([P, 4, 16, 8, 4], BF16, name="grouped", align_bytes=64)
+            grouped[n] = grp.tile([P, 4, 32, 4, 4], BF16, name="grouped", align_bytes=64)
             if shares(n)[3]:
                 src, dst = lay(n, 3)
                 nc.gpsimd.tensor_scalar(out=dst, in0=src, scalar1=1.0, scalar2=0.0, op0=ALU.mult, op1=ALU.add)
 
         def interleave_v(n):
-            src, dst = lay(n, 0)
+            src, dst = (ap.rearrange("p s j r i -> p s j i r") for ap in lay(n, 0))
             nc.vector.tensor_copy(out=dst, in_=src)
 
         id_ps = {}
@@ -208,7 +210,7 @@ def tile_temporalaugmentedbilinear_t_kernel(tc, x_bytes, x_scale, w1, g, w, w2, 
             id_ps[n] = ps_i.tile([P, 256], BF16, name="id_ps")
             nc.tensor.matmul(
                 id_ps[n][:].rearrange("p (t i) -> p t i", i=4), lhsT=ident_b[:],
-                rhs=src.rearrange("p a j r i -> p (a j r) i"), start=True, stop=True,
+                rhs=src.rearrange("p s j r i -> p (s j r) i"), start=True, stop=True,
             )
 
         def interleave_s(n):
@@ -217,8 +219,8 @@ def tile_temporalaugmentedbilinear_t_kernel(tc, x_bytes, x_scale, w1, g, w, w2, 
             if shares(n)[2]:
                 src, dst = lay(n, 2)
                 nc.scalar.copy(
-                    out=dst.rearrange("p a j r i -> p a j (r i)"),
-                    in_=id_ps[n][:].rearrange("p (a j c) -> p a j c", j=4, c=32),
+                    out=dst.rearrange("p s j r i -> p s j (r i)"),
+                    in_=id_ps[n][:].rearrange("p (s j c) -> p s j c", j=4, c=16),
                 )
             if shares(n)[1]:
                 src, dst = lay(n, 1)
@@ -229,7 +231,7 @@ def tile_temporalaugmentedbilinear_t_kernel(tc, x_bytes, x_scale, w1, g, w, w2, 
             xsc[n] = cod.tile([P, 512], U8, name="xsc", align_bytes=64)
             nc.vector.quantize_mx(
                 out=xc[n][:].bitcast(FP8X4), scales=xsc[n][:],
-                in_=grouped[n][:].rearrange("p j a r i -> p (j a r i)"),
+                in_=grouped[n][:].rearrange("p j s r i -> p (j s r i)"),
             )
 
         h_ps = {}
@@ -278,7 +280,7 @@ def tile_temporalaugmentedbilinear_t_kernel(tc, x_bytes, x_scale, w1, g, w, w2, 
                     start=True, stop=True,
                 )
 
-        mn, sm, rs, cc, ks, ex = {}, {}, {}, {}, {}, {}
+        mn, sm, dd, cc, ks, ex = {}, {}, {}, {}, {}, {}
 
         def row_max(q):
             mn[q] = ep.tile([P, 2], F32, name="mn")
@@ -294,12 +296,14 @@ def tile_temporalaugmentedbilinear_t_kernel(tc, x_bytes, x_scale, w1, g, w, w2, 
                 )
 
         def factors(q):
-            rs[q] = ep.tile([P, 2], F32, name="rs")
-            cc[q] = ep.tile([P, 2], F32, name="cc")
+            dd[q] = ep.tile([P, 2], F32, name="dd")
             ks[q] = ep.tile([P, 2], F32, name="ks")
+            nc.gpsimd.tensor_scalar(out=dd[q][:], in0=sm[q][:], scalar1=rc[:, 0:1], scalar2=None, op0=ALU.mult)
             nc.gpsimd.tensor_scalar(out=ks[q][:], in0=sm[q][:], scalar1=kk[:, 0:1], scalar2=None, op0=ALU.mult)
-            nc.vector.reciprocal(rs[q][:], sm[q][:])
-            nc.gpsimd.tensor_scalar(out=cc[q][:], in0=rs[q][:], scalar1=c128[:, 0:1], scalar2=None, op0=ALU.mult)
+
+        def invert(q):
+            cc[q] = ep.tile([P, 2], F32, name="cc")
+            nc.vector.reciprocal(cc[q][:], dd[q][:])
 
         def weigh(q):
             for r in (0, 1):
@@ -342,16 +346,17 @@ def tile_temporalaugmentedbilinear_t_kernel(tc, x_bytes, x_scale, w1, g, w, w2, 
                 quant(n - 1)
                 mm1(n - 1)
             interleave_g(n + 2)
+            at(factors, 7, n)
             interleave_t(n + 2)
             interleave_s(n + 1)
-            if n + AHEAD < B:
-                widen_half(n + AHEAD)
             if 0 <= n - 2 < B:
                 gain(n - 2)
+            at(invert, 8, n)
             at(weigh, 8, n)
             at(row_max, 5, n)
             at(mix, 9, n)
-            at(factors, 7, n)
+            if n + AHEAD < B:
+                widen_half(n + AHEAD)
             at(exps, 6, n)
             at(hquant, 4, n)
             at(mm2, 4, n)

@@ -26,6 +26,8 @@ def shares(n):
         return 32, 0, 0, 0
     if n >= 28:
         return 2, 20, 4, 6
+    if n % 2 == 0:
+        return 20, 0, 4, 8
     return 22, 0, 4, 6
 
 
@@ -52,28 +54,31 @@ def tile_temporalaugmentedbilinear_t_kernel(tc, x_bytes, x_scale, w1, g, w, w2, 
             q = b // 2
             if b % 2 == 0:
                 raw[q] = raws.tile([P, 4, 2, T], U8, name="raw", align_bytes=64)
-            nc.sync.dma_start(out=raw[q][:, :, b % 2, :], in_=x_bytes[b].rearrange("(p i) t -> p i t", i=4))
+            rows = x_bytes[b].rearrange("(p i) t -> p i t", i=4)
+            for i in ((2, 0) if b == 0 else (0,)):
+                k = 2 if b == 0 else 4
+                nc.sync.dma_start(out=raw[q][:, i : i + k, b % 2, :], in_=rows[:, i : i + k])
 
         xs = keep.tile([P, 4], F32, name="xs")
         nc.sync.dma_start(out=xs[:], in_=x_scale.rearrange("o (p i) z -> p (o i z)", i=4))
         load(0)
-        load(1)
 
         w1_sb = keep.tile([P, D], BF16, name="w1_sb", align_bytes=64)
         w_sb = keep.tile([P, 2, 4, Q], BF16, name="w_sb", align_bytes=64)
         g_sb = keep.tile([P, 4], BF16, name="g_sb")
         lam_sb = keep.tile([P, 1], BF16, name="lam_sb")
         bias_sb = keep.tile([P, Q], BF16, name="bias_sb")
-        nc.scalar.dma_start(out=w1_sb[:], in_=w1)
+        nc.sync.dma_start(out=w1_sb[:], in_=w1)
+        load(1)
         g_rows = keep.tile([P, P], BF16, name="g_rows", align_bytes=64)
         nc.gpsimd.memset(g_rows[:], 0.0)
         nc.scalar.dma_start(
             out=g_rows[0:4, :].rearrange("j (s r) -> j s r", r=4), in_=g.rearrange("(s j r) -> j s r", j=4, r=4)
         )
         nc.scalar.dma_start(out=lam_sb[:], in_=lam.rearrange("(p o) -> p o", o=1))
-        nc.scalar.dma_start(out=bias_sb[:], in_=bias)
         for b in range(2, 6):
             load(b)
+        nc.sync.dma_start(out=bias_sb[:], in_=bias)
         for k, wt in enumerate((w2, w)):
             rows = wt.rearrange("(s j r) q -> r s j q", j=4, r=4)
             for r in range(4):
@@ -104,7 +109,7 @@ def tile_temporalaugmentedbilinear_t_kernel(tc, x_bytes, x_scale, w1, g, w, w2, 
             for i in (2 * (h % 2), 2 * (h % 2) + 1):
                 wide = planes[q][:, i].rearrange("p b t -> p (b t)")
                 codes = raw[q][:, i].rearrange("p b t -> p (b t)").bitcast(FP8)
-                if i == 3 and q % 3 == 2:
+                if (q == 1 and i % 2) or (q % 4 == 3 and i == 3):
                     nc.vector.tensor_scalar(out=wide, in0=codes, scalar1=xs[:, i : i + 1], scalar2=None, op0=ALU.mult)
                 else:
                     nc.scalar.activation(out=wide, in_=codes, func=ACT.Copy, scale=xs[:, i : i + 1])
@@ -166,7 +171,7 @@ def tile_temporalaugmentedbilinear_t_kernel(tc, x_bytes, x_scale, w1, g, w, w2, 
         c128 = keep.tile([P, 1], F32, name="c128")
         oml = keep.tile([P, 1], F32, name="oml")
         rc = keep.tile([P, 1], F32, name="rc")
-        kk = keep.tile([P, 1], F32, name="kk")
+        coef = keep.tile([P, 2], F32, name="coef")
         TINY = 1e-20
 
         def prep_lam():
@@ -177,7 +182,8 @@ def tile_temporalaugmentedbilinear_t_kernel(tc, x_bytes, x_scale, w1, g, w, w2, 
             nc.gpsimd.tensor_scalar(out=c128[:], in0=c128[:], scalar1=128.0, scalar2=None, op0=ALU.mult)
             nc.gpsimd.tensor_scalar(out=oml[:], in0=lam_sb[:], scalar1=-1.0, scalar2=1.0, op0=ALU.mult, op1=ALU.add)
             nc.vector.reciprocal(rc[:], c128[:])
-            nc.gpsimd.tensor_tensor(out=kk[:], in0=oml[:], in1=rc[:], op=ALU.mult)
+            nc.gpsimd.tensor_copy(out=coef[:, 0:1], in_=rc[:])
+            nc.gpsimd.tensor_tensor(out=coef[:, 1:2], in0=oml[:], in1=rc[:], op=ALU.mult)
 
         grouped, xc, xsc = {}, {}, {}
 
@@ -280,7 +286,7 @@ def tile_temporalaugmentedbilinear_t_kernel(tc, x_bytes, x_scale, w1, g, w, w2, 
                     start=True, stop=True,
                 )
 
-        mn, sm, dd, cc, ks, ex = {}, {}, {}, {}, {}, {}
+        mn, sm, fac, cc, ex = {}, {}, {}, {}, {}
 
         def row_max(q):
             mn[q] = ep.tile([P, 2], F32, name="mn")
@@ -296,19 +302,20 @@ def tile_temporalaugmentedbilinear_t_kernel(tc, x_bytes, x_scale, w1, g, w, w2, 
                 )
 
         def factors(q):
-            dd[q] = ep.tile([P, 2], F32, name="dd")
-            ks[q] = ep.tile([P, 2], F32, name="ks")
-            nc.gpsimd.tensor_scalar(out=dd[q][:], in0=sm[q][:], scalar1=rc[:, 0:1], scalar2=None, op0=ALU.mult)
-            nc.gpsimd.tensor_scalar(out=ks[q][:], in0=sm[q][:], scalar1=kk[:, 0:1], scalar2=None, op0=ALU.mult)
+            fac[q] = ep.tile([P, 2, 2], F32, name="fac")
+            nc.gpsimd.tensor_tensor(
+                out=fac[q][:], in0=sm[q][:].unsqueeze(1).to_broadcast([P, 2, 2]),
+                in1=coef[:].unsqueeze(2).to_broadcast([P, 2, 2]), op=ALU.mult,
+            )
 
         def invert(q):
             cc[q] = ep.tile([P, 2], F32, name="cc")
-            nc.vector.reciprocal(cc[q][:], dd[q][:])
+            nc.vector.reciprocal(cc[q][:], fac[q][:, 0])
 
         def weigh(q):
             for r in (0, 1):
                 nc.vector.scalar_tensor_tensor(
-                    out=ex[q][:, r], in0=ex[q][:, r], scalar=ks[q][:, r : r + 1], in1=ue[q][:, r, 0],
+                    out=ex[q][:, r], in0=ex[q][:, r], scalar=fac[q][:, 1, r : r + 1], in1=ue[q][:, r, 0],
                     op0=ALU.add, op1=ALU.mult,
                 )
 
@@ -332,6 +339,9 @@ def tile_temporalaugmentedbilinear_t_kernel(tc, x_bytes, x_scale, w1, g, w, w2, 
         interleave_g(1)
         for n in range(B + 9):
             load(n + LOAD_AHEAD)
+            if 0 <= n - 1 < B:
+                quant(n - 1)
+                mm1(n - 1)
             if n < B:
                 interleave_v(n)
             if n == 0:
@@ -342,9 +352,6 @@ def tile_temporalaugmentedbilinear_t_kernel(tc, x_bytes, x_scale, w1, g, w, w2, 
                 prep_w_copy()
             if n == 3:
                 prep_w_quant()
-            if 0 <= n - 1 < B:
-                quant(n - 1)
-                mm1(n - 1)
             interleave_g(n + 2)
             at(factors, 7, n)
             interleave_t(n + 2)

from contextlib import ExitStack

import concourse.mybir as mybir
from concourse.masks import make_identity

B, D, T, PF, Q = 32, 512, 512, 128, 128
FLOPS = 2 * B * PF * D * T + 2 * 2 * B * PF * T * Q

F32 = mybir.dt.float32
BF16 = mybir.dt.bfloat16
U32 = mybir.dt.uint32
U8 = mybir.dt.uint8
FP8 = mybir.dt.float8_e4m3fn
FP8X4 = mybir.dt.float8_e4m3fn_x4
ALU = mybir.AluOpType
ACT = mybir.ActivationFunctionType
AX = mybir.AxisListType

P = 128
AHEAD = 5
LOAD_AHEAD = 10


def shares(n):
    if n < 2:
        return 32, 0, 0, 0
    if n >= 28:
        return 2, 20, 4, 6
    if n % 2 == 0:
        return 20, 0, 4, 8
    return 22, 0, 4, 6


def tile_temporalaugmentedbilinear_t_kernel(tc, x_bytes, x_scale, w1, g, w, w2, lam, bias, out):
    nc = tc.nc
    with ExitStack() as ctx:
        keep = ctx.enter_context(tc.tile_pool(name="keep", bufs=1))
        raws = ctx.enter_context(tc.tile_pool(name="raws", bufs=6))
        pln = ctx.enter_context(tc.tile_pool(name="pln", bufs=4))
        grp = ctx.enter_context(tc.tile_pool(name="grp", bufs=3))
        cod = ctx.enter_context(tc.tile_pool(name="cod", bufs=3))
        hp = ctx.enter_context(tc.tile_pool(name="hp", bufs=2))
        ep = ctx.enter_context(tc.tile_pool(name="ep", bufs=4))
        ps_h = ctx.enter_context(tc.psum_pool(name="ps_h", bufs=3))
        ps_ue = ctx.enter_context(tc.psum_pool(name="ps_ue", bufs=3))
        ps_i = ctx.enter_context(tc.psum_pool(name="ps_i", bufs=2))
        ctx.enter_context(tc.manual_schedule())

        raw = {}

        def load(b):
            if b >= B:
                return
            q = b // 2
            if b % 2 == 0:
                raw[q] = raws.tile([P, 4, 2, T], U8, name="raw", align_bytes=64)
            rows = x_bytes[b].rearrange("(p i) t -> p i t", i=4)
            for i in ((2, 0) if b == 0 else (0,)):
                k = 2 if b == 0 else 4
                nc.sync.dma_start(out=raw[q][:, i : i + k, b % 2, :], in_=rows[:, i : i + k])

        xs = keep.tile([P, 4], F32, name="xs")
        nc.sync.dma_start(out=xs[:], in_=x_scale.rearrange("o (p i) z -> p (o i z)", i=4))
        load(0)

        w1_sb = keep.tile([P, D], BF16, name="w1_sb", align_bytes=64)
        w_sb = keep.tile([P, 2, 4, Q], BF16, name="w_sb", align_bytes=64)
        g_sb = keep.tile([P, 4], BF16, name="g_sb")
        lam_sb = keep.tile([P, 1], BF16, name="lam_sb")
        bias_sb = keep.tile([P, Q], BF16, name="bias_sb")
        nc.sync.dma_start(out=w1_sb[:], in_=w1)
        load(1)
        g_rows = keep.tile([P, P], BF16, name="g_rows", align_bytes=64)
        nc.gpsimd.memset(g_rows[:], 0.0)
        nc.scalar.dma_start(
            out=g_rows[0:4, :].rearrange("j (s r) -> j s r", r=4), in_=g.rearrange("(s j r) -> j s r", j=4, r=4)
        )
        nc.scalar.dma_start(out=lam_sb[:], in_=lam.rearrange("(p o) -> p o", o=1))
        for b in range(2, 6):
            load(b)
        nc.sync.dma_start(out=bias_sb[:], in_=bias)
        for k, wt in enumerate((w2, w)):
            rows = wt.rearrange("(s j r) q -> r s j q", j=4, r=4)
            for r in range(4):
                nc.sync.dma_start(out=w_sb[r:P:4, k], in_=rows[r])
        for b in range(6, LOAD_AHEAD):
            load(b)

        warm = keep.tile([P, 1], F32, name="warm")
        nc.gpsimd.memset(warm[:], 0.0)
        nc.scalar.activation(out=warm[:], in_=warm[:], func=ACT.Exp)

        ident = keep.tile([P, P], F32, name="ident")
        make_identity(nc, ident[:])
        ident_b = keep.tile([P, P], BF16, name="ident_b", align_bytes=64)
        nc.gpsimd.tensor_copy(out=ident_b[:], in_=ident[:])

        planes = {}

        def new_planes(q):
            planes[q] = pln.tile([P, 4, 2, T], BF16, name="planes", align_bytes=64)

        def widen_half(h):
            if h >= B:
                return
            q = h // 2
            if h % 2 == 0:
                new_planes(q)
            for i in (2 * (h % 2), 2 * (h % 2) + 1):
                wide = planes[q][:, i].rearrange("p b t -> p (b t)")
                codes = raw[q][:, i].rearrange("p b t -> p (b t)").bitcast(FP8)
                if (q == 1 and i % 2) or (q % 4 == 3 and i == 3):
                    nc.vector.tensor_scalar(out=wide, in0=codes, scalar1=xs[:, i : i + 1], scalar2=None, op0=ALU.mult)
                else:
                    nc.scalar.activation(out=wide, in_=codes, func=ACT.Copy, scale=xs[:, i : i + 1])

        new_planes(0)
        for b in (0, 1):
            for i in range(4):
                if i < 2:
                    nc.vector.tensor_scalar(
                        out=planes[0][:, i, b, :], in0=raw[0][:, i, b, :].bitcast(FP8),
                        scalar1=xs[:, i : i + 1], scalar2=None, op0=ALU.mult,
                    )
                else:
                    nc.scalar.activation(
                        out=planes[0][:, i, b, :], in_=raw[0][:, i, b, :].bitcast(FP8),
                        func=ACT.Copy, scale=xs[:, i : i + 1],
                    )
        for h in range(2, AHEAD):
            widen_half(h)

        w1_words = w1_sb[:].bitcast(F32)
        w1_t = ps_h.tile([P, 512], F32, name="h_ps")
        for u in (0, 1):
            nc.tensor.transpose(w1_t[:, 128 * u : 128 * (u + 1)], w1_words[:, u : 256 : 2], ident[:])
        w1_g = keep.tile([P, 512], BF16, name="w1_g", align_bytes=64)
        w1_c = keep.tile([P, 128], U32, name="w1_c", align_bytes=64)
        w1_s = keep.tile([P, 128], U8, name="w1_s", align_bytes=64)
        w_g = keep.tile([P, 2, Q, 4], BF16, name="w_g", align_bytes=64)
        w_c = keep.tile([P, 256], U32, name="w_c", align_bytes=64)
        w_s = keep.tile([P, 256], U8, name="w_s", align_bytes=64)

        g_t = ps_i.tile([P, P], BF16, name="id_ps")
        nc.tensor.transpose(g_t[:], g_rows[:], ident_b[:])

        def prep_w1_copy():
            nc.vector.tensor_copy(out=g_sb[:], in_=g_t[:, 0:4])
            nc.vector.tensor_copy(
                out=w1_g[:].bitcast(F32).rearrange("p (r u) -> p r u", u=2),
                in_=w1_t[:, 0:256].rearrange("p (u r) -> p r u", u=2),
            )

        def prep_w1_quant():
            nc.vector.quantize_mx(out=w1_c[:].bitcast(FP8X4), scales=w1_s[:], in_=w1_g[:])

        def prep_w_copy():
            nc.vector.tensor_copy(out=w_g[:, 0], in_=w_sb[:, 0].rearrange("p j q -> p q j"))
            nc.vector.tensor_scalar(
                out=w_g[:, 1], in0=w_sb[:, 1].rearrange("p j q -> p q j"),
                scalar1=-1.0, scalar2=None, op0=ALU.mult,
            )

        def prep_w_quant():
            nc.vector.quantize_mx(
                out=w_c[:].bitcast(FP8X4), scales=w_s[:], in_=w_g[:].rearrange("p a q j -> p (a q j)")
            )

        lam_lo = keep.tile([P, 1], F32, name="lam_lo")
        lam_hi = keep.tile([P, 1], F32, name="lam_hi")
        c128 = keep.tile([P, 1], F32, name="c128")
        oml = keep.tile([P, 1], F32, name="oml")
        rc = keep.tile([P, 1], F32, name="rc")
        coef = keep.tile([P, 2], F32, name="coef")
        TINY = 1e-20

        def prep_lam():
            nc.gpsimd.tensor_scalar(out=lam_lo[:], in0=lam_sb[:], scalar1=TINY, scalar2=TINY, op0=ALU.is_lt, op1=ALU.mult)
            nc.gpsimd.tensor_scalar(out=lam_hi[:], in0=lam_sb[:], scalar1=-TINY, scalar2=None, op0=ALU.is_gt)
            nc.gpsimd.tensor_tensor(out=lam_lo[:], in0=lam_lo[:], in1=lam_hi[:], op=ALU.mult)
            nc.gpsimd.tensor_tensor(out=c128[:], in0=lam_lo[:], in1=lam_sb[:], op=ALU.add)
            nc.gpsimd.tensor_scalar(out=c128[:], in0=c128[:], scalar1=128.0, scalar2=None, op0=ALU.mult)
            nc.gpsimd.tensor_scalar(out=oml[:], in0=lam_sb[:], scalar1=-1.0, scalar2=1.0, op0=ALU.mult, op1=ALU.add)
            nc.vector.reciprocal(rc[:], c128[:])
            nc.gpsimd.tensor_copy(out=coef[:, 0:1], in_=rc[:])
            nc.gpsimd.tensor_tensor(out=coef[:, 1:2], in0=oml[:], in1=rc[:], op=ALU.mult)

        grouped, xc, xsc = {}, {}, {}

        def lay(n, part):
            s = shares(n)
            a0 = sum(s[:part])
            a1 = a0 + s[part]
            src = planes[n // 2][:, :, n % 2, :].rearrange("p i (s j r) -> p s j r i", j=4, r=4)
            dst = grouped[n][:].rearrange("p j s r i -> p s j r i")
            return src[:, a0:a1], dst[:, a0:a1]

        def interleave_g(n):
            if n >= B:
                return
            grouped[n] = grp.tile([P, 4, 32, 4, 4], BF16, name="grouped", align_bytes=64)
            if shares(n)[3]:
                src, dst = lay(n, 3)
                nc.gpsimd.tensor_scalar(out=dst, in0=src, scalar1=1.0, scalar2=0.0, op0=ALU.mult, op1=ALU.add)

        def interleave_v(n):
            src, dst = (ap.rearrange("p s j r i -> p s j i r") for ap in lay(n, 0))
            nc.vector.tensor_copy(out=dst, in_=src)

        id_ps = {}

        def interleave_t(n):
            if n >= B or not shares(n)[2]:
                return
            src, dst = lay(n, 2)
            id_ps[n] = ps_i.tile([P, 256], BF16, name="id_ps")
            nc.tensor.matmul(
                id_ps[n][:].rearrange("p (t i) -> p t i", i=4), lhsT=ident_b[:],
                rhs=src.rearrange("p s j r i -> p (s j r) i"), start=True, stop=True,
            )

        def interleave_s(n):
            if n >= B:
                return
            if shares(n)[2]:
                src, dst = lay(n, 2)
                nc.scalar.copy(
                    out=dst.rearrange("p s j r i -> p s j (r i)"),
                    in_=id_ps[n][:].rearrange("p (s j c) -> p s j c", j=4, c=16),
                )
            if shares(n)[1]:
                src, dst = lay(n, 1)
                nc.scalar.copy(out=dst, in_=src)

        def quant(n):
            xc[n] = cod.tile([P, 512], U32, name="xc", align_bytes=64)
            xsc[n] = cod.tile([P, 512], U8, name="xsc", align_bytes=64)
            nc.vector.quantize_mx(
                out=xc[n][:].bitcast(FP8X4), scales=xsc[n][:],
                in_=grouped[n][:].rearrange("p j s r i -> p (j s r i)"),
            )

        h_ps = {}

        def mm1(n):
            h_ps[n] = ps_h.tile([P, 512], F32, name="h_ps")
            for j in range(4):
                cols = slice(128 * j, 128 * (j + 1))
                nc.tensor.matmul_mx(
                    out=h_ps[n][:, cols],
                    lhsT=xc[n][:, cols].bitcast(FP8X4), lhsT_scale=xsc[n][:, cols],
                    rhs=w1_c[:].bitcast(FP8X4), rhs_scale=w1_s[:],
                    start=True, stop=True,
                )

        hg, hc, hs = {}, {}, {}

        def gain(n):
            q = n // 2
            if n % 2 == 0:
                hg[q] = hp.tile([P, 2, PF, 4], BF16, name="hg", align_bytes=64)
            nc.vector.tensor_tensor(
                out=hg[q][:, n % 2],
                in0=h_ps[n][:].rearrange("p (j f) -> p f j", j=4),
                in1=g_sb[:].unsqueeze(1).to_broadcast([P, PF, 4]),
                op=ALU.mult,
            )

        def hquant(q):
            hc[q] = hp.tile([P, 2 * PF], U32, name="hc", align_bytes=64)
            hs[q] = hp.tile([P, 2 * PF], U8, name="hs", align_bytes=64)
            nc.vector.quantize_mx(
                out=hc[q][:].bitcast(FP8X4), scales=hs[q][:], in_=hg[q][:].rearrange("p b f j -> p (b f j)")
            )

        ue = {}

        def mm2(q):
            ue[q] = ps_ue.tile([P, 2, 2, Q], F32, name="ue")
            for r in (0, 1):
                rows = slice(PF * r, PF * (r + 1))
                nc.tensor.matmul_mx(
                    out=ue[q][:, r].rearrange("p a q -> p (a q)"),
                    lhsT=hc[q][:, rows].bitcast(FP8X4), lhsT_scale=hs[q][:, rows],
                    rhs=w_c[:].bitcast(FP8X4), rhs_scale=w_s[:],
                    start=True, stop=True,
                )

        mn, sm, fac, cc, ex = {}, {}, {}, {}, {}

        def row_max(q):
            mn[q] = ep.tile([P, 2], F32, name="mn")
            nc.vector.tensor_reduce(out=mn[q][:], in_=ue[q][:, :, 1], axis=AX.X, op=ALU.min)

        def exps(q):
            sm[q] = ep.tile([P, 2], F32, name="sm")
            ex[q] = ep.tile([P, 2, Q], F32, name="ex")
            for r in (0, 1):
                nc.scalar.activation(
                    out=ex[q][:, r], in_=ue[q][:, r, 1], func=ACT.Exp,
                    bias=mn[q][:, r : r + 1], scale=-1.0, accum_out=sm[q][:, r : r + 1],
                )

        def factors(q):
            fac[q] = ep.tile([P, 2, 2], F32, name="fac")
            nc.gpsimd.tensor_tensor(
                out=fac[q][:], in0=sm[q][:].unsqueeze(1).to_broadcast([P, 2, 2]),
                in1=coef[:].unsqueeze(2).to_broadcast([P, 2, 2]), op=ALU.mult,
            )

        def invert(q):
            cc[q] = ep.tile([P, 2], F32, name="cc")
            nc.vector.reciprocal(cc[q][:], fac[q][:, 0])

        def weigh(q):
            for r in (0, 1):
                nc.vector.scalar_tensor_tensor(
                    out=ex[q][:, r], in0=ex[q][:, r], scalar=fac[q][:, 1, r : r + 1], in1=ue[q][:, r, 0],
                    op0=ALU.add, op1=ALU.mult,
                )

        def mix(q):
            for r in (0, 1):
                nc.vector.scalar_tensor_tensor(
                    out=ex[q][:, r], in0=ex[q][:, r], scalar=cc[q][:, r : r + 1], in1=bias_sb[:],
                    op0=ALU.mult, op1=ALU.add,
                )

        def finish(q):
            o = ep.tile([P, 2, Q], F32, name="o")
            nc.scalar.activation(out=o[:], in_=ex[q][:], func=ACT.Tanh)
            nc.sync.dma_start(out=out[2 * q : 2 * q + 2].rearrange("b p q -> p b q"), in_=o[:])

        def at(stage, lag, n):
            if 0 <= n - lag < B and (n - lag) % 2 == 0:
                stage((n - lag) // 2)

        interleave_g(0)
        interleave_g(1)
        for n in range(B + 9):
            load(n + LOAD_AHEAD)
            if 0 <= n - 1 < B:
                quant(n - 1)
                mm1(n - 1)
            if n < B:
                interleave_v(n)
            if n == 0:
                prep_w1_copy()
                prep_w1_quant()
                prep_lam()
            if n == 2:
                prep_w_copy()
            if n == 3:
                prep_w_quant()
            interleave_g(n + 2)
            at(factors, 7, n)
            interleave_t(n + 2)
            interleave_s(n + 1)
            if 0 <= n - 2 < B:
                gain(n - 2)
            at(invert, 8, n)
            at(weigh, 8, n)
            at(row_max, 5, n)
            at(mix, 9, n)
            if n + AHEAD < B:
                widen_half(n + AHEAD)
            at(exps, 6, n)
            at(hquant, 4, n)
            at(mm2, 4, n)
            at(finish, 10, n)
